import numpy as np
import ml_dtypes


def mxq(x, axis, fmt="e4m3"):
    dtype, down = {"e4m3": (ml_dtypes.float8_e4m3fn, 7), "e5m2": (ml_dtypes.float8_e5m2, 14)}[fmt]
    v = np.moveaxis(np.asarray(x, np.float32).astype(ml_dtypes.bfloat16).astype(np.float64), axis, -1)
    blocks = v.reshape(v.shape[:-1] + (-1, 32))
    amax = np.abs(blocks).max(-1, keepdims=True)
    byte = np.maximum(np.where(amax > 0, np.frexp(amax)[1] - 1 + 127, 0) - down, 1)
    scale = np.exp2(byte - 127.0)
    codes = (blocks / scale).astype(np.float32).astype(dtype).astype(np.float64)
    return np.moveaxis((codes * scale).reshape(v.shape), -1, axis)


WIDE = False


def mx_kscale(k):
    if not WIDE:
        return np.ones(k)
    levels = np.array([10, -10, 5, -5, 0])
    if k % 512:
        return np.exp2(np.random.permutation(np.resize(levels, k // 32))).repeat(32)
    a = np.empty((k // 512, 16))
    for p in range(k // 512):
        a[p, :8] = np.random.permutation(np.resize(levels, 8))
        for g in range(8):
            far = levels[np.abs(levels - a[p, g]) >= 10]
            a[p, g + 8] = far[np.random.randint(len(far))]
    return np.exp2(a.ravel()).repeat(32)


def f64(x):
    return np.asarray(x).astype(np.float64)


def striped8(idx):
    return np.asarray(idx).reshape(8, -1, 16).transpose(0, 2, 1).reshape(128, -1).astype(np.uint16)


def unstriped8(offs):
    return offs.reshape(8, 16, -1).transpose(0, 2, 1).reshape(8, -1).astype(np.int64)


def pick8(x, idx, run):
    r = np.arange(len(x))
    return x[r[:, None], idx[r % (8 * run) // run]]


E2M1 = np.array([0.0, 0.5, 1.0, 1.5, 2.0, 3.0, 4.0, 6.0, -0.0, -0.5, -1.0, -1.5, -2.0, -3.0, -4.0, -6.0])


def pack_weight(w, fmt):
    k, n = w.shape
    w = f64(np.asarray(w, np.float32).astype(ml_dtypes.bfloat16)).reshape(k // 32, 32, n)
    amax = np.abs(w).max(1)
    if fmt == "e4m3":
        byte = np.frexp(amax)[1] - 1 + 127 - 7
    else:
        mant, ex = np.frexp(amax / 6.0)
        byte = np.where(mant > 0.5, ex, ex - 1) + 127
    byte = np.clip(np.where(amax > 0, byte, 1), 1, 254)
    scaled = (w * np.exp2(127.0 - byte)[:, None, :]).reshape(k, n).astype(np.float32)
    by_word = np.ascontiguousarray(scaled.reshape(k // 512, 128, 4, n).transpose(0, 1, 3, 2))
    if fmt == "e4m3":
        words = by_word.astype(ml_dtypes.float8_e4m3fn).view(np.uint8)
    else:
        c = by_word.astype(ml_dtypes.float4_e2m1fn).view(np.uint8) & 0xF
        words = (c[..., 0::2] | (c[..., 1::2] << 4)).reshape(k // 512, 128, 2 * n)
    return np.ascontiguousarray(words), np.ascontiguousarray(byte.astype(np.uint8).reshape(k // 512, 16, n))


def unpack_weight(words, scales, fmt):
    g, _, n = scales.shape
    words = np.ascontiguousarray(words).reshape(g, 128, n, -1)
    if fmt == "e4m3":
        vals = words.view(ml_dtypes.float8_e4m3fn).astype(np.float64)
    else:
        nib = np.empty((g, 128, n, 4), np.uint8)
        nib[..., 0::2] = words & 0xF
        nib[..., 1::2] = words >> 4
        vals = E2M1[nib]
    vals = vals * np.repeat(np.exp2(scales.astype(np.float64) - 127.0), 8, axis=1)[..., None]
    return vals.transpose(0, 1, 3, 2).reshape(g * 512, n)


def softplus(v):
    return np.log(1.0 + np.exp(v))


def sigmoid(v):
    return 1.0 / (1.0 + np.exp(-v))


D, E, T, Q, I = 512, 512, 1024, 128, 512


def setup_inputs():
    n = np.random.standard_normal
    idx = np.stack([np.random.permutation(T)[:I] for _ in range(8)])
    fd = mx_kscale(D)
    fe = mx_kscale(E)
    keysp = pack_weight(n((D, T)) / fd[:, None], "e4m3")
    return {
        "query": (n((D, Q)) * 1.0 / np.sqrt(D) * fd[:, None]).astype(np.float32),
        "keys_words": keysp[0],
        "keys_scales": keysp[1],
        "gout": (n((E, Q)) * 1 / np.sqrt(E) * fe[:, None]).astype(np.float32),
        "vals": (n((E, T)) / fe[:, None]).astype(np.float32),
        "th": (np.random.uniform(-0.5, 0.5, (Q, 1))).astype(np.float32),
        "reserve": (np.random.uniform(20.0, 60.0, (Q, 1))).astype(np.float32),
        "old": (0.5 * n((Q, T))).astype(np.float32),
        "offs": striped8(idx),
    }


def reference(query, keys_words, keys_scales, gout, vals, th, reserve, old, offs):
    idx = unstriped8(offs)
    keysu = unpack_weight(keys_words, keys_scales, "e4m3")
    queryq = mxq(f64(query), 0, "e4m3")
    a = queryq.T @ keysu
    p = softplus(pick8(a, idx, 16) - f64(th))
    z = np.sum(p, axis=1, keepdims=True) + f64(reserve)
    goutq = mxq(f64(gout), 0, "e4m3")
    valsq = mxq(f64(vals), 0, "e4m3")
    c0 = goutq.T @ valsq
    dw = pick8(c0, idx, 16)
    dz = np.sum(dw * p / np.square(z) * (-1.0), axis=1, keepdims=True)
    dp = dw / z + dz
    e1 = dp * sigmoid(pick8(a, idx, 16) - f64(th))
    s1 = np.zeros((Q, T))
    s1[np.arange(Q)[:, None], idx[np.arange(Q) % 128 // 16]] = e1
    y = s1 * 1024.0 + f64(old)
    return y

@@ -1,0 +1,152 @@
+from contextlib import ExitStack
+
+import concourse.mybir as mybir
+
+F32 = mybir.dt.float32
+BF16 = mybir.dt.bfloat16
+I32 = mybir.dt.int32
+U32 = mybir.dt.uint32
+U16 = mybir.dt.uint16
+U8 = mybir.dt.uint8
+FP8X4 = mybir.dt.float8_e4m3fn_x4
+ALU = mybir.AluOpType
+ACT = mybir.ActivationFunctionType
+
+P = 128
+PACK = 4
+T = 1024
+SLOTS = 512
+BANK = 512
+OUT_SCALE = 1024.0
+LN_FLOOR = 2.0 ** -63
+VALS_CHUNKS = (256, 512, 256)
+FLOPS = 2 * 2 * 128 * 512 * 1024
+
+
+def interleave(copy, grouped, raw):
+    copy(
+        out=grouped[:].rearrange("p (c i) j -> p c j i", i=4),
+        in_=raw[:].rearrange("p j (c i) -> p c j i", i=4),
+    )
+
+
+def quantize(nc, codes, scales, grouped):
+    nc.vector.quantize_mx(out=codes[:].bitcast(FP8X4), scales=scales[:], in_=grouped[:].rearrange("p w j -> p (w j)"))
+
+
+def tile_attend_bspotlight_heads_kernel(tc, query, keys_words, keys_scales, gout, vals, th, reserve, old, offs, out):
+    nc = tc.nc
+    last = len(VALS_CHUNKS) - 1
+    with ExitStack() as ctx:
+        sb = ctx.enter_context(tc.tile_pool(name="sb", bufs=1))
+        ps = ctx.enter_context(tc.psum_pool(name="ps", bufs=1))
+
+        offsets = sb.tile([P, SLOTS // 16], U16, name="offsets")
+        k_scales = sb.tile([P, T], U8, name="k_scales", align_bytes=64)
+        k_codes = sb.tile([P, T], U32, name="k_codes", align_bytes=64)
+        nc.vector.memset(k_scales[:].bitcast(I32), 0)
+        for quad in range(4):
+            nc.scalar.dma_start(
+                out=k_scales[32 * quad : 32 * quad + 4, :].bitcast(I32),
+                in_=keys_scales[0, 4 * quad : 4 * quad + 4, :].bitcast(I32),
+            )
+        warm_in = sb.tile([P, 1], F32, name="warm_in")
+        warm_out = sb.tile([P, 1], F32, name="warm_out")
+        nc.vector.memset(warm_in[:], 0.0)
+        nc.scalar.activation(warm_out[:], warm_in[:], ACT.Sigmoid)
+
+        th_col = sb.tile([P, 1], F32, name="th_col")
+        res_col = sb.tile([P, 1], F32, name="res_col")
+        nc.gpsimd.dma_start(out=th_col[:], in_=th)
+        nc.gpsimd.dma_start(out=res_col[:], in_=reserve)
+        q_raw = sb.tile([P, PACK, P], F32, name="q_raw")
+        nc.sync.dma_start(out=q_raw[:], in_=query.rearrange("(p j) w -> p j w", j=PACK))
+        nc.sync.dma_start(out=k_codes[:].bitcast(I32), in_=keys_words[0].rearrange("p n t -> p (n t)").bitcast(I32))
+        nc.sync.dma_start(offsets[:], offs)
+        g_raw = sb.tile([P, PACK, P], F32, name="g_raw")
+        nc.sync.dma_start(out=g_raw[:], in_=gout.rearrange("(p j) w -> p j w", j=PACK))
+        vals_rows = vals.rearrange("(p j) w -> p j w", j=PACK)
+        starts = [sum(VALS_CHUNKS[:c]) for c in range(len(VALS_CHUNKS))]
+        v_raw = [sb.tile([P, PACK, w], F32, name="v_raw%d" % c, align_bytes=64) for c, w in enumerate(VALS_CHUNKS)]
+        old_sb = sb.tile([P, T], F32, name="old_sb")
+        for c, w in enumerate(VALS_CHUNKS):
+            nc.sync.dma_start(out=v_raw[c][:], in_=vals_rows[:, :, starts[c] : starts[c] + w])
+        nc.sync.dma_start(out=old_sb[:], in_=old)
+
+        scattered = sb.tile([P, T], F32, name="scattered")
+        nc.vector.memset(scattered[:], 0.0)
+
+        q_grouped = sb.tile([P, P, PACK], BF16, name="q_grouped", align_bytes=64)
+        q_codes = sb.tile([P, P], U32, name="q_codes", align_bytes=64)
+        q_scales = sb.tile([P, P], U8, name="q_scales", align_bytes=64)
+        interleave(nc.vector.tensor_copy, q_grouped, q_raw)
+        quantize(nc, q_codes, q_scales, q_grouped)
+        g_grouped = sb.tile([P, P, PACK], BF16, name="g_grouped", align_bytes=64)
+        g_codes = sb.tile([P, P], U32, name="g_codes", align_bytes=64)
+        g_scales = sb.tile([P, P], U8, name="g_scales", align_bytes=64)
+        interleave(nc.vector.tensor_copy, g_grouped, g_raw)
+        quantize(nc, g_codes, g_scales, g_grouped)
+        neg_th = sb.tile([P, 1], F32, name="neg_th")
+        nc.vector.tensor_scalar(neg_th[:], th_col[:], -1.0, None, ALU.mult)
+        neg_a = sb.tile([P, SLOTS + 8], F32, name="neg_a")
+        ln_sig_neg = sb.tile([P, SLOTS + 8], F32, name="ln_sig_neg")
+        nc.vector.memset(neg_a[:, SLOTS : SLOTS + 1], 2.0 ** 100)
+        nc.vector.tensor_scalar(ln_sig_neg[:, SLOTS : SLOTS + 1], res_col[:], -1.0, None, ALU.mult)
+
+        a = sb.tile([P, T], F32, name="a", tag="a", align_bytes=64)
+        for h in range(2):
+            cols = slice(h * BANK, (h + 1) * BANK)
+            a_ps = ps.tile([P, BANK], F32, name="a_ps%d" % h)
+            nc.tensor.matmul_mx(
+                out=a_ps[:], lhsT=q_codes[:].bitcast(FP8X4), lhsT_scale=q_scales[:],
+                rhs=k_codes[:, cols].bitcast(FP8X4), rhs_scale=k_scales[:, cols], start=True, stop=True,
+            )
+            [nc.scalar.copy, nc.vector.tensor_copy][h](out=a[:, cols], in_=a_ps[:])
+
+        nc.vector.tensor_scalar(neg_a[:, 0:SLOTS], a[:].indirect(offsets[:]), -1.0, 0.0, ALU.mult, ALU.add)
+
+        il = [nc.scalar.copy, nc.vector.tensor_copy, nc.vector.tensor_copy]
+        ev = [nc.scalar.copy] * 3
+        c_ps = []
+        for c, w in enumerate(VALS_CHUNKS):
+            v_grouped = sb.tile([P, w, PACK], BF16, name="v_grouped%d" % c, tag="vg%d" % c, align_bytes=64)
+            v_codes = sb.tile([P, w], U32, name="v_codes%d" % c, tag="a" if c == 0 else "vc%d" % c, align_bytes=64)
+            v_scales = sb.tile([P, w], U8, name="v_scales%d" % c, align_bytes=64)
+            interleave(il[c], v_grouped, v_raw[c])
+            quantize(nc, v_codes, v_scales, v_grouped)
+            c_ps.append(ps.tile([P, BANK], F32, name="c_ps%d" % c))
+            nc.tensor.matmul_mx(
+                out=c_ps[c][:, 0:w], lhsT=g_codes[:].bitcast(FP8X4), lhsT_scale=g_scales[:],
+                rhs=v_codes[:].bitcast(FP8X4), rhs_scale=v_scales[:], start=True, stop=True,
+            )
+
+        sig_neg = sb.tile([P, SLOTS], F32, name="sig_neg", tag="v_raw0", align_bytes=64)
+        sig = sb.tile([P, SLOTS], F32, name="sig")
+        nc.scalar.activation(sig[:], neg_a[:, 0:SLOTS], ACT.Sigmoid, bias=neg_th[:], scale=-1.0)
+        nc.scalar.activation(sig_neg[:], neg_a[:, 0:SLOTS], ACT.Sigmoid, bias=th_col[:])
+        nc.scalar.activation(ln_sig_neg[:, 0:SLOTS], sig_neg[:], ACT.Ln, bias=LN_FLOOR)
+
+        c0 = sb.tile([P, T], F32, name="c0", tag="v_raw0", align_bytes=64)
+        for c, w in enumerate(VALS_CHUNKS):
+            ev[c](out=c0[:, starts[c] : starts[c] + w], in_=c_ps[c][:, 0:w])
+
+        neg_p = sb.tile([P, SLOTS + 8], F32, name="neg_p", tag="vg%d" % last, align_bytes=64)
+        neg_sum = sb.tile([P, 1], F32, name="neg_sum")
+        inv_z = sb.tile([P, 1], F32, name="inv_z")
+        ext = slice(0, SLOTS + 1)
+        nc.vector.scalar_tensor_tensor(neg_p[:, ext], neg_a[:, ext], th_col[:], ln_sig_neg[:, ext], ALU.add, ALU.min, accum_out=neg_sum[:])
+        nc.vector.reciprocal(inv_z[:], neg_sum[:])
+
+        dw = sb.tile([P, SLOTS], F32, name="dw", tag="dw", align_bytes=64)
+        nc.vector.tensor_copy(dw[:], c0[:].indirect(offsets[:]))
+        weighted = sb.tile([P, SLOTS], F32, name="weighted")
+        neg_mean = sb.tile([P, 1], F32, name="neg_mean")
+        nc.vector.scalar_tensor_tensor(weighted[:], dw[:], inv_z[:], neg_p[:, 0:SLOTS], ALU.mult, ALU.mult, accum_out=neg_mean[:])
+        dp = sb.tile([P, SLOTS], F32, name="dp")
+        nc.vector.tensor_scalar(dp[:], dw[:], neg_mean[:], inv_z[:], ALU.subtract, ALU.mult)
+        nc.vector.tensor_tensor(scattered[:].indirect(offsets[:]), dp[:], sig[:], ALU.mult)
+
+        for h, (lo, hi) in enumerate([(0, 512), (512, 768), (768, 1024)]):
+            y = sb.tile([P, hi - lo], F32, name="y%d" % h)
+            nc.vector.scalar_tensor_tensor(y[:], scattered[:, lo:hi], -OUT_SCALE, old_sb[:, lo:hi], ALU.mult, ALU.add)
+            [nc.sync, nc.scalar][h % 2].dma_start(out=out[:, lo:hi], in_=y[:])

@@ -19,14 +19,15 @@ SLOTS = 512
 BANK = 512
 OUT_SCALE = 1024.0
 LN_FLOOR = 2.0 ** -63
-VALS_CHUNKS = (256, 512, 256)
+VALS_CHUNKS = (128, 256, 256, 256, 128)
+A_PIECE = 256
 FLOPS = 2 * 2 * 128 * 512 * 1024
 
 
 def interleave(copy, grouped, raw):
     copy(
-        out=grouped[:].rearrange("p (c i) j -> p c j i", i=4),
-        in_=raw[:].rearrange("p j (c i) -> p c j i", i=4),
+        out=grouped.rearrange("p (c i) j -> p c j i", i=4),
+        in_=raw.rearrange("p j (c i) -> p c j i", i=4),
     )
 
 
@@ -44,109 +45,132 @@ def tile_attend_bspotlight_heads_kernel(tc, query, keys_words, keys_scales, gout
         offsets = sb.tile([P, SLOTS // 16], U16, name="offsets")
         k_scales = sb.tile([P, T], U8, name="k_scales", align_bytes=64)
         k_codes = sb.tile([P, T], U32, name="k_codes", align_bytes=64)
-        nc.vector.memset(k_scales[:].bitcast(I32), 0)
         for quad in range(4):
             nc.scalar.dma_start(
                 out=k_scales[32 * quad : 32 * quad + 4, :].bitcast(I32),
                 in_=keys_scales[0, 4 * quad : 4 * quad + 4, :].bitcast(I32),
             )
+        th_col = sb.tile([P, 1], F32, name="th_col")
+        nc.scalar.dma_start(out=th_col[:], in_=th)
         warm_in = sb.tile([P, 1], F32, name="warm_in")
         warm_out = sb.tile([P, 1], F32, name="warm_out")
         nc.vector.memset(warm_in[:], 0.0)
         nc.scalar.activation(warm_out[:], warm_in[:], ACT.Sigmoid)
 
-        th_col = sb.tile([P, 1], F32, name="th_col")
         res_col = sb.tile([P, 1], F32, name="res_col")
-        nc.gpsimd.dma_start(out=th_col[:], in_=th)
-        nc.gpsimd.dma_start(out=res_col[:], in_=reserve)
         q_raw = sb.tile([P, PACK, P], F32, name="q_raw")
-        nc.sync.dma_start(out=q_raw[:], in_=query.rearrange("(p j) w -> p j w", j=PACK))
-        nc.sync.dma_start(out=k_codes[:].bitcast(I32), in_=keys_words[0].rearrange("p n t -> p (n t)").bitcast(I32))
-        nc.sync.dma_start(offsets[:], offs)
         g_raw = sb.tile([P, PACK, P], F32, name="g_raw")
-        nc.sync.dma_start(out=g_raw[:], in_=gout.rearrange("(p j) w -> p j w", j=PACK))
         vals_rows = vals.rearrange("(p j) w -> p j w", j=PACK)
         starts = [sum(VALS_CHUNKS[:c]) for c in range(len(VALS_CHUNKS))]
         v_raw = [sb.tile([P, PACK, w], F32, name="v_raw%d" % c, align_bytes=64) for c, w in enumerate(VALS_CHUNKS)]
         old_sb = sb.tile([P, T], F32, name="old_sb")
-        for c, w in enumerate(VALS_CHUNKS):
-            nc.sync.dma_start(out=v_raw[c][:], in_=vals_rows[:, :, starts[c] : starts[c] + w])
+
+        def load_vals(c):
+            nc.sync.dma_start(out=v_raw[c][:], in_=vals_rows[:, :, starts[c] : starts[c] + VALS_CHUNKS[c]])
+
+        nc.sync.dma_start(out=q_raw[:], in_=query.rearrange("(p j) w -> p j w", j=PACK))
+        nc.sync.dma_start(out=k_codes[:].bitcast(I32), in_=keys_words[0].rearrange("p n t -> p (n t)").bitcast(I32))
+        nc.sync.dma_start(out=g_raw[:], in_=gout.rearrange("(p j) w -> p j w", j=PACK))
+        nc.sync.dma_start(offsets[:], offs)
+        load_vals(0)
+        load_vals(1)
+        load_vals(2)
+        load_vals(3)
+        load_vals(4)
+        nc.sync.dma_start(out=res_col[:], in_=reserve)
         nc.sync.dma_start(out=old_sb[:], in_=old)
 
         scattered = sb.tile([P, T], F32, name="scattered")
         nc.vector.memset(scattered[:], 0.0)
+        neg_a = sb.tile([P, SLOTS + 8], F32, name="neg_a")
+        ln_sig_neg = sb.tile([P, SLOTS + 8], F32, name="ln_sig_neg")
+        nc.vector.memset(neg_a[:, SLOTS : SLOTS + 1], 2.0 ** 100)
 
         q_grouped = sb.tile([P, P, PACK], BF16, name="q_grouped", align_bytes=64)
         q_codes = sb.tile([P, P], U32, name="q_codes", align_bytes=64)
         q_scales = sb.tile([P, P], U8, name="q_scales", align_bytes=64)
-        interleave(nc.vector.tensor_copy, q_grouped, q_raw)
+        interleave(nc.vector.tensor_copy, q_grouped[:], q_raw[:])
         quantize(nc, q_codes, q_scales, q_grouped)
         g_grouped = sb.tile([P, P, PACK], BF16, name="g_grouped", align_bytes=64)
         g_codes = sb.tile([P, P], U32, name="g_codes", align_bytes=64)
         g_scales = sb.tile([P, P], U8, name="g_scales", align_bytes=64)
-        interleave(nc.vector.tensor_copy, g_grouped, g_raw)
+        interleave(nc.vector.tensor_copy, g_grouped[:], g_raw[:])
         quantize(nc, g_codes, g_scales, g_grouped)
-        neg_th = sb.tile([P, 1], F32, name="neg_th")
-        nc.vector.tensor_scalar(neg_th[:], th_col[:], -1.0, None, ALU.mult)
-        neg_a = sb.tile([P, SLOTS + 8], F32, name="neg_a")
-        ln_sig_neg = sb.tile([P, SLOTS + 8], F32, name="ln_sig_neg")
-        nc.vector.memset(neg_a[:, SLOTS : SLOTS + 1], 2.0 ** 100)
-        nc.vector.tensor_scalar(ln_sig_neg[:, SLOTS : SLOTS + 1], res_col[:], -1.0, None, ALU.mult)
 
         a = sb.tile([P, T], F32, name="a", tag="a", align_bytes=64)
-        for h in range(2):
-            cols = slice(h * BANK, (h + 1) * BANK)
+        a_ev = [nc.scalar.copy] * 4
+        for h in range(T // A_PIECE):
+            cols = slice(h * A_PIECE, (h + 1) * A_PIECE)
             a_ps = ps.tile([P, BANK], F32, name="a_ps%d" % h)
             nc.tensor.matmul_mx(
-                out=a_ps[:], lhsT=q_codes[:].bitcast(FP8X4), lhsT_scale=q_scales[:],
+                out=a_ps[:, 0:A_PIECE], lhsT=q_codes[:].bitcast(FP8X4), lhsT_scale=q_scales[:],
                 rhs=k_codes[:, cols].bitcast(FP8X4), rhs_scale=k_scales[:, cols], start=True, stop=True,
             )
-            [nc.scalar.copy, nc.vector.tensor_copy][h](out=a[:, cols], in_=a_ps[:])
+            a_ev[h](out=a[:, cols], in_=a_ps[:, 0:A_PIECE])
 
         nc.vector.tensor_scalar(neg_a[:, 0:SLOTS], a[:].indirect(offsets[:]), -1.0, 0.0, ALU.mult, ALU.add)
 
-        il = [nc.scalar.copy, nc.vector.tensor_copy, nc.vector.tensor_copy]
-        ev = [nc.scalar.copy] * 3
+        il = [[(nc.vector.tensor_copy, 0, 128)], [(nc.scalar.copy, 0, 256)], [(nc.vector.tensor_copy, 0, 256)], [(nc.vector.tensor_copy, 0, 256)], [(nc.vector.tensor_copy, 0, 128)]]
+        ev = [nc.scalar.copy] * 4
         c_ps = []
-        for c, w in enumerate(VALS_CHUNKS):
-            v_grouped = sb.tile([P, w, PACK], BF16, name="v_grouped%d" % c, tag="vg%d" % c, align_bytes=64)
-            v_codes = sb.tile([P, w], U32, name="v_codes%d" % c, tag="a" if c == 0 else "vc%d" % c, align_bytes=64)
+        v_grouped = []
+
+        def group(c):
+            w = VALS_CHUNKS[c]
+            v_grouped.append(sb.tile([P, w, PACK], BF16, name="v_grouped%d" % c, tag="vg%d" % c, align_bytes=64))
+            for copy, lo, hi in il[c]:
+                interleave(copy, v_grouped[c][:, lo:hi, :], v_raw[c][:, :, lo:hi])
+
+        def multiply(c):
+            w = VALS_CHUNKS[c]
+            v_codes = sb.tile([P, w], U32, name="v_codes%d" % c, tag="vc%d" % c, align_bytes=64)
             v_scales = sb.tile([P, w], U8, name="v_scales%d" % c, align_bytes=64)
-            interleave(il[c], v_grouped, v_raw[c])
-            quantize(nc, v_codes, v_scales, v_grouped)
-            c_ps.append(ps.tile([P, BANK], F32, name="c_ps%d" % c))
+            quantize(nc, v_codes, v_scales, v_grouped[c])
+            if c != 1:
+                c_ps.append(ps.tile([P, BANK], F32, name="c_ps%d" % c))
+            at = VALS_CHUNKS[0] if c == 1 else 0
             nc.tensor.matmul_mx(
-                out=c_ps[c][:, 0:w], lhsT=g_codes[:].bitcast(FP8X4), lhsT_scale=g_scales[:],
+                out=c_ps[-1][:, at : at + w], lhsT=g_codes[:].bitcast(FP8X4), lhsT_scale=g_scales[:],
                 rhs=v_codes[:].bitcast(FP8X4), rhs_scale=v_scales[:], start=True, stop=True,
             )
 
-        sig_neg = sb.tile([P, SLOTS], F32, name="sig_neg", tag="v_raw0", align_bytes=64)
-        sig = sb.tile([P, SLOTS], F32, name="sig")
-        nc.scalar.activation(sig[:], neg_a[:, 0:SLOTS], ACT.Sigmoid, bias=neg_th[:], scale=-1.0)
+        for c in range(last + 1):
+            group(c)
+            multiply(c)
+
+        sig_neg = sb.tile([P, SLOTS], F32, name="sig_neg", tag="v_raw1", align_bytes=64)
         nc.scalar.activation(sig_neg[:], neg_a[:, 0:SLOTS], ACT.Sigmoid, bias=th_col[:])
         nc.scalar.activation(ln_sig_neg[:, 0:SLOTS], sig_neg[:], ACT.Ln, bias=LN_FLOOR)
 
-        c0 = sb.tile([P, T], F32, name="c0", tag="v_raw0", align_bytes=64)
-        for c, w in enumerate(VALS_CHUNKS):
-            ev[c](out=c0[:, starts[c] : starts[c] + w], in_=c_ps[c][:, 0:w])
+        c0 = sb.tile([P, T], F32, name="c0", tag="v_raw1", align_bytes=64)
+        edges = [0] + starts[2:] + [T]
+        for b, bank in enumerate(c_ps):
+            ev[b](out=c0[:, edges[b] : edges[b + 1]], in_=bank[:, 0 : edges[b + 1] - edges[b]])
 
-        neg_p = sb.tile([P, SLOTS + 8], F32, name="neg_p", tag="vg%d" % last, align_bytes=64)
-        neg_sum = sb.tile([P, 1], F32, name="neg_sum")
-        inv_z = sb.tile([P, 1], F32, name="inv_z")
+        neg_th = sb.tile([P, 1], F32, name="neg_th")
+        nc.vector.tensor_scalar(neg_th[:], th_col[:], -1.0, 0.0, ALU.mult, ALU.add)
+        nc.vector.tensor_scalar(ln_sig_neg[:, SLOTS : SLOTS + 1], res_col[:], -1.0, 0.0, ALU.mult, ALU.add)
+        sig = sb.tile([P, SLOTS], F32, name="sig", tag="vc%d" % last, align_bytes=64)
+        nc.scalar.activation(sig[:], neg_a[:, 0:SLOTS], ACT.Sigmoid, bias=neg_th[:], scale=-1.0)
+
+        neg_p = sb.tile([P, SLOTS + 8], F32, name="neg_p", tag="v_raw%d" % last, align_bytes=64)
+        neg_z = sb.tile([P, 1], F32, name="neg_z")
+        neg_inv_z = sb.tile([P, 1], F32, name="neg_inv_z")
         ext = slice(0, SLOTS + 1)
-        nc.vector.scalar_tensor_tensor(neg_p[:, ext], neg_a[:, ext], th_col[:], ln_sig_neg[:, ext], ALU.add, ALU.min, accum_out=neg_sum[:])
-        nc.vector.reciprocal(inv_z[:], neg_sum[:])
+        nc.vector.scalar_tensor_tensor(neg_p[:, ext], neg_a[:, ext], th_col[:], ln_sig_neg[:, ext], ALU.add, ALU.min, accum_out=neg_z[:])
+        nc.vector.reciprocal(neg_inv_z[:], neg_z[:])
 
         dw = sb.tile([P, SLOTS], F32, name="dw", tag="dw", align_bytes=64)
         nc.vector.tensor_copy(dw[:], c0[:].indirect(offsets[:]))
         weighted = sb.tile([P, SLOTS], F32, name="weighted")
-        neg_mean = sb.tile([P, 1], F32, name="neg_mean")
-        nc.vector.scalar_tensor_tensor(weighted[:], dw[:], inv_z[:], neg_p[:, 0:SLOTS], ALU.mult, ALU.mult, accum_out=neg_mean[:])
+        mean = sb.tile([P, 1], F32, name="mean")
+        nc.vector.scalar_tensor_tensor(weighted[:], dw[:], neg_inv_z[:], neg_p[:, 0:SLOTS], ALU.mult, ALU.mult, accum_out=mean[:])
         dp = sb.tile([P, SLOTS], F32, name="dp")
-        nc.vector.tensor_scalar(dp[:], dw[:], neg_mean[:], inv_z[:], ALU.subtract, ALU.mult)
+        nc.vector.tensor_scalar(dp[:], dw[:], mean[:], neg_inv_z[:], ALU.subtract, ALU.mult)
         nc.vector.tensor_tensor(scattered[:].indirect(offsets[:]), dp[:], sig[:], ALU.mult)
+        final_scale = -OUT_SCALE
 
-        for h, (lo, hi) in enumerate([(0, 512), (512, 768), (768, 1024)]):
+        for h, (lo, hi) in enumerate([(0, 512), (512, 1024)]):
             y = sb.tile([P, hi - lo], F32, name="y%d" % h)
-            nc.vector.scalar_tensor_tensor(y[:], scattered[:, lo:hi], -OUT_SCALE, old_sb[:, lo:hi], ALU.mult, ALU.add)
+            nc.vector.scalar_tensor_tensor(y[:], scattered[:, lo:hi], final_scale, old_sb[:, lo:hi], ALU.mult, ALU.add)
             [nc.sync, nc.scalar][h % 2].dma_start(out=out[:, lo:hi], in_=y[:])

@@ -16,28 +16,39 @@ P = 128
 PACK = 4
 T = 1024
 SLOTS = 512
+PADDED_SLOTS = SLOTS + 8
 BANK = 512
 OUT_SCALE = 1024.0
-LN_FLOOR = 2.0 ** -63
+LN_FLOOR = 2.0**-63
+NEVER_THE_MINIMUM = 2.0**100
+
+SCORE_PIECE = 256
 VALS_CHUNKS = (128, 256, 256, 256, 128)
-A_PIECE = 256
-FLOPS = 2 * 2 * 128 * 512 * 1024
+SCALAR_CHUNK = 1
+STORE_PIECE = 512
+
+FLOPS = 2 * 2 * P * (P * PACK) * T
 
 
 def interleave(copy, grouped, raw):
     copy(
-        out=grouped.rearrange("p (c i) j -> p c j i", i=4),
-        in_=raw.rearrange("p j (c i) -> p c j i", i=4),
+        out=grouped[:].rearrange("p (c i) j -> p c j i", i=4),
+        in_=raw[:].rearrange("p j (c i) -> p c j i", i=4),
     )
 
 
 def quantize(nc, codes, scales, grouped):
-    nc.vector.quantize_mx(out=codes[:].bitcast(FP8X4), scales=scales[:], in_=grouped[:].rearrange("p w j -> p (w j)"))
+    nc.vector.quantize_mx(out=codes[:].bitcast(FP8X4), scales=scales[:], in_=grouped[:].rearrange("p c j -> p (c j)"))
 
 
 def tile_attend_bspotlight_heads_kernel(tc, query, keys_words, keys_scales, gout, vals, th, reserve, old, offs, out):
     nc = tc.nc
-    last = len(VALS_CHUNKS) - 1
+    last_chunk = len(VALS_CHUNKS) - 1
+    chunk_starts = [sum(VALS_CHUNKS[:c]) for c in range(len(VALS_CHUNKS))]
+    listed = slice(0, SLOTS)
+    reserve_column = slice(SLOTS, SLOTS + 1)
+    listed_and_reserve = slice(0, SLOTS + 1)
+
     with ExitStack() as ctx:
         sb = ctx.enter_context(tc.tile_pool(name="sb", bufs=1))
         ps = ctx.enter_context(tc.psum_pool(name="ps", bufs=1))
@@ -45,132 +56,134 @@ def tile_attend_bspotlight_heads_kernel(tc, query, keys_words, keys_scales, gout
         offsets = sb.tile([P, SLOTS // 16], U16, name="offsets")
         k_scales = sb.tile([P, T], U8, name="k_scales", align_bytes=64)
         k_codes = sb.tile([P, T], U32, name="k_codes", align_bytes=64)
-        for quad in range(4):
+        for quadrant in range(4):
             nc.scalar.dma_start(
-                out=k_scales[32 * quad : 32 * quad + 4, :].bitcast(I32),
-                in_=keys_scales[0, 4 * quad : 4 * quad + 4, :].bitcast(I32),
+                out=k_scales[32 * quadrant : 32 * quadrant + 4, :].bitcast(I32),
+                in_=keys_scales[0, 4 * quadrant : 4 * quadrant + 4, :].bitcast(I32),
             )
         th_col = sb.tile([P, 1], F32, name="th_col")
         nc.scalar.dma_start(out=th_col[:], in_=th)
+
         warm_in = sb.tile([P, 1], F32, name="warm_in")
         warm_out = sb.tile([P, 1], F32, name="warm_out")
         nc.vector.memset(warm_in[:], 0.0)
         nc.scalar.activation(warm_out[:], warm_in[:], ACT.Sigmoid)
 
-        res_col = sb.tile([P, 1], F32, name="res_col")
+        reserve_col = sb.tile([P, 1], F32, name="reserve_col")
         q_raw = sb.tile([P, PACK, P], F32, name="q_raw")
         g_raw = sb.tile([P, PACK, P], F32, name="g_raw")
-        vals_rows = vals.rearrange("(p j) w -> p j w", j=PACK)
-        starts = [sum(VALS_CHUNKS[:c]) for c in range(len(VALS_CHUNKS))]
         v_raw = [sb.tile([P, PACK, w], F32, name="v_raw%d" % c, align_bytes=64) for c, w in enumerate(VALS_CHUNKS)]
         old_sb = sb.tile([P, T], F32, name="old_sb")
-
-        def load_vals(c):
-            nc.sync.dma_start(out=v_raw[c][:], in_=vals_rows[:, :, starts[c] : starts[c] + VALS_CHUNKS[c]])
-
-        nc.sync.dma_start(out=q_raw[:], in_=query.rearrange("(p j) w -> p j w", j=PACK))
-        nc.sync.dma_start(out=k_codes[:].bitcast(I32), in_=keys_words[0].rearrange("p n t -> p (n t)").bitcast(I32))
-        nc.sync.dma_start(out=g_raw[:], in_=gout.rearrange("(p j) w -> p j w", j=PACK))
+        nc.sync.dma_start(out=q_raw[:], in_=query.rearrange("(p j) c -> p j c", j=PACK))
+        nc.sync.dma_start(out=k_codes[:].bitcast(I32), in_=keys_words[0].rearrange("p c j -> p (c j)").bitcast(I32))
+        nc.sync.dma_start(out=g_raw[:], in_=gout.rearrange("(p j) c -> p j c", j=PACK))
         nc.sync.dma_start(offsets[:], offs)
-        load_vals(0)
-        load_vals(1)
-        load_vals(2)
-        load_vals(3)
-        load_vals(4)
-        nc.sync.dma_start(out=res_col[:], in_=reserve)
+        vals_rows = vals.rearrange("(p j) c -> p j c", j=PACK)
+        for c, w in enumerate(VALS_CHUNKS):
+            nc.sync.dma_start(out=v_raw[c][:], in_=vals_rows[:, :, chunk_starts[c] : chunk_starts[c] + w])
+        nc.sync.dma_start(out=reserve_col[:], in_=reserve)
         nc.sync.dma_start(out=old_sb[:], in_=old)
 
-        scattered = sb.tile([P, T], F32, name="scattered")
-        nc.vector.memset(scattered[:], 0.0)
-        neg_a = sb.tile([P, SLOTS + 8], F32, name="neg_a")
-        ln_sig_neg = sb.tile([P, SLOTS + 8], F32, name="ln_sig_neg")
-        nc.vector.memset(neg_a[:, SLOTS : SLOTS + 1], 2.0 ** 100)
+        neg_s1 = sb.tile([P, T], F32, name="neg_s1")
+        nc.vector.memset(neg_s1[:], 0.0)
+        neg_a = sb.tile([P, PADDED_SLOTS], F32, name="neg_a")
+        ln_sigmoid = sb.tile([P, PADDED_SLOTS], F32, name="ln_sigmoid")
+        nc.vector.memset(neg_a[:, reserve_column], NEVER_THE_MINIMUM)
 
         q_grouped = sb.tile([P, P, PACK], BF16, name="q_grouped", align_bytes=64)
         q_codes = sb.tile([P, P], U32, name="q_codes", align_bytes=64)
         q_scales = sb.tile([P, P], U8, name="q_scales", align_bytes=64)
-        interleave(nc.vector.tensor_copy, q_grouped[:], q_raw[:])
+        interleave(nc.vector.tensor_copy, q_grouped, q_raw)
         quantize(nc, q_codes, q_scales, q_grouped)
         g_grouped = sb.tile([P, P, PACK], BF16, name="g_grouped", align_bytes=64)
         g_codes = sb.tile([P, P], U32, name="g_codes", align_bytes=64)
         g_scales = sb.tile([P, P], U8, name="g_scales", align_bytes=64)
-        interleave(nc.vector.tensor_copy, g_grouped[:], g_raw[:])
+        interleave(nc.vector.tensor_copy, g_grouped, g_raw)
         quantize(nc, g_codes, g_scales, g_grouped)
 
-        a = sb.tile([P, T], F32, name="a", tag="a", align_bytes=64)
-        a_ev = [nc.scalar.copy] * 4
-        for h in range(T // A_PIECE):
-            cols = slice(h * A_PIECE, (h + 1) * A_PIECE)
-            a_ps = ps.tile([P, BANK], F32, name="a_ps%d" % h)
+        a = sb.tile([P, T], F32, name="a", align_bytes=64)
+        for piece in range(T // SCORE_PIECE):
+            cols = slice(piece * SCORE_PIECE, (piece + 1) * SCORE_PIECE)
+            a_bank = ps.tile([P, BANK], F32, name="a_bank%d" % piece)
             nc.tensor.matmul_mx(
-                out=a_ps[:, 0:A_PIECE], lhsT=q_codes[:].bitcast(FP8X4), lhsT_scale=q_scales[:],
-                rhs=k_codes[:, cols].bitcast(FP8X4), rhs_scale=k_scales[:, cols], start=True, stop=True,
+                out=a_bank[:, 0:SCORE_PIECE],
+                lhsT=q_codes[:].bitcast(FP8X4),
+                lhsT_scale=q_scales[:],
+                rhs=k_codes[:, cols].bitcast(FP8X4),
+                rhs_scale=k_scales[:, cols],
+                start=True,
+                stop=True,
             )
-            a_ev[h](out=a[:, cols], in_=a_ps[:, 0:A_PIECE])
+            copy = nc.vector.tensor_copy if piece == 0 else nc.scalar.copy
+            copy(out=a[:, cols], in_=a_bank[:, 0:SCORE_PIECE])
 
-        nc.vector.tensor_scalar(neg_a[:, 0:SLOTS], a[:].indirect(offsets[:]), -1.0, 0.0, ALU.mult, ALU.add)
+        nc.vector.tensor_scalar(neg_a[:, listed], a[:].indirect(offsets[:]), -1.0, 0.0, ALU.mult, ALU.add)
 
-        il = [[(nc.vector.tensor_copy, 0, 128)], [(nc.scalar.copy, 0, 256)], [(nc.vector.tensor_copy, 0, 256)], [(nc.vector.tensor_copy, 0, 256)], [(nc.vector.tensor_copy, 0, 128)]]
-        ev = [nc.scalar.copy] * 4
-        c_ps = []
-        v_grouped = []
-
-        def group(c):
-            w = VALS_CHUNKS[c]
-            v_grouped.append(sb.tile([P, w, PACK], BF16, name="v_grouped%d" % c, tag="vg%d" % c, align_bytes=64))
-            for copy, lo, hi in il[c]:
-                interleave(copy, v_grouped[c][:, lo:hi, :], v_raw[c][:, :, lo:hi])
-
-        def multiply(c):
-            w = VALS_CHUNKS[c]
-            v_codes = sb.tile([P, w], U32, name="v_codes%d" % c, tag="vc%d" % c, align_bytes=64)
+        c_banks = []
+        bank_starts = []
+        for c, w in enumerate(VALS_CHUNKS):
+            v_grouped = sb.tile([P, w, PACK], BF16, name="v_grouped%d" % c, align_bytes=64)
+            interleave(nc.scalar.copy if c == SCALAR_CHUNK else nc.vector.tensor_copy, v_grouped, v_raw[c])
+            v_codes = sb.tile([P, w], U32, name="v_codes%d" % c, align_bytes=64)
             v_scales = sb.tile([P, w], U8, name="v_scales%d" % c, align_bytes=64)
-            quantize(nc, v_codes, v_scales, v_grouped[c])
-            if c != 1:
-                c_ps.append(ps.tile([P, BANK], F32, name="c_ps%d" % c))
-            at = VALS_CHUNKS[0] if c == 1 else 0
+            quantize(nc, v_codes, v_scales, v_grouped)
+            if c != SCALAR_CHUNK:
+                c_banks.append(ps.tile([P, BANK], F32, name="c_bank%d" % c))
+                bank_starts.append(chunk_starts[c])
+            at = chunk_starts[c] - bank_starts[-1]
             nc.tensor.matmul_mx(
-                out=c_ps[-1][:, at : at + w], lhsT=g_codes[:].bitcast(FP8X4), lhsT_scale=g_scales[:],
-                rhs=v_codes[:].bitcast(FP8X4), rhs_scale=v_scales[:], start=True, stop=True,
+                out=c_banks[-1][:, at : at + w],
+                lhsT=g_codes[:].bitcast(FP8X4),
+                lhsT_scale=g_scales[:],
+                rhs=v_codes[:].bitcast(FP8X4),
+                rhs_scale=v_scales[:],
+                start=True,
+                stop=True,
             )
 
-        for c in range(last + 1):
-            group(c)
-            multiply(c)
+        sigmoid_neg_x = sb.tile([P, SLOTS], F32, name="sigmoid_neg_x", tag="v_raw%d" % SCALAR_CHUNK, align_bytes=64)
+        nc.scalar.activation(sigmoid_neg_x[:], neg_a[:, listed], ACT.Sigmoid, bias=th_col[:])
+        nc.scalar.activation(ln_sigmoid[:, listed], sigmoid_neg_x[:], ACT.Ln, bias=LN_FLOOR)
 
-        sig_neg = sb.tile([P, SLOTS], F32, name="sig_neg", tag="v_raw1", align_bytes=64)
-        nc.scalar.activation(sig_neg[:], neg_a[:, 0:SLOTS], ACT.Sigmoid, bias=th_col[:])
-        nc.scalar.activation(ln_sig_neg[:, 0:SLOTS], sig_neg[:], ACT.Ln, bias=LN_FLOOR)
-
-        c0 = sb.tile([P, T], F32, name="c0", tag="v_raw1", align_bytes=64)
-        edges = [0] + starts[2:] + [T]
-        for b, bank in enumerate(c_ps):
-            ev[b](out=c0[:, edges[b] : edges[b + 1]], in_=bank[:, 0 : edges[b + 1] - edges[b]])
+        c0 = sb.tile([P, T], F32, name="c0", align_bytes=64)
+        for bank, lo, hi in zip(c_banks, bank_starts, bank_starts[1:] + [T]):
+            nc.scalar.copy(out=c0[:, lo:hi], in_=bank[:, 0 : hi - lo])
 
         neg_th = sb.tile([P, 1], F32, name="neg_th")
         nc.vector.tensor_scalar(neg_th[:], th_col[:], -1.0, 0.0, ALU.mult, ALU.add)
-        nc.vector.tensor_scalar(ln_sig_neg[:, SLOTS : SLOTS + 1], res_col[:], -1.0, 0.0, ALU.mult, ALU.add)
-        sig = sb.tile([P, SLOTS], F32, name="sig", tag="vc%d" % last, align_bytes=64)
-        nc.scalar.activation(sig[:], neg_a[:, 0:SLOTS], ACT.Sigmoid, bias=neg_th[:], scale=-1.0)
+        nc.vector.tensor_scalar(ln_sigmoid[:, reserve_column], reserve_col[:], -1.0, 0.0, ALU.mult, ALU.add)
 
-        neg_p = sb.tile([P, SLOTS + 8], F32, name="neg_p", tag="v_raw%d" % last, align_bytes=64)
+        neg_p = sb.tile([P, PADDED_SLOTS], F32, name="neg_p", tag="v_grouped%d" % last_chunk, align_bytes=64)
         neg_z = sb.tile([P, 1], F32, name="neg_z")
         neg_inv_z = sb.tile([P, 1], F32, name="neg_inv_z")
-        ext = slice(0, SLOTS + 1)
-        nc.vector.scalar_tensor_tensor(neg_p[:, ext], neg_a[:, ext], th_col[:], ln_sig_neg[:, ext], ALU.add, ALU.min, accum_out=neg_z[:])
-        nc.vector.reciprocal(neg_inv_z[:], neg_z[:])
+        nc.vector.scalar_tensor_tensor(
+            neg_p[:, listed_and_reserve],
+            neg_a[:, listed_and_reserve],
+            th_col[:],
+            ln_sigmoid[:, listed_and_reserve],
+            ALU.add,
+            ALU.min,
+            accum_out=neg_z[:],
+        )
 
-        dw = sb.tile([P, SLOTS], F32, name="dw", tag="dw", align_bytes=64)
+        sigmoid_x = sb.tile([P, SLOTS], F32, name="sigmoid_x", tag="ln_sigmoid")
+        nc.scalar.activation(sigmoid_x[:], neg_a[:, listed], ACT.Sigmoid, bias=neg_th[:], scale=-1.0)
+
+        dw = sb.tile([P, SLOTS], F32, name="dw", align_bytes=64)
         nc.vector.tensor_copy(dw[:], c0[:].indirect(offsets[:]))
-        weighted = sb.tile([P, SLOTS], F32, name="weighted")
+        nc.vector.reciprocal(neg_inv_z[:], neg_z[:])
+        weighted_dw = sb.tile([P, SLOTS], F32, name="weighted_dw")
         mean = sb.tile([P, 1], F32, name="mean")
-        nc.vector.scalar_tensor_tensor(weighted[:], dw[:], neg_inv_z[:], neg_p[:, 0:SLOTS], ALU.mult, ALU.mult, accum_out=mean[:])
-        dp = sb.tile([P, SLOTS], F32, name="dp")
-        nc.vector.tensor_scalar(dp[:], dw[:], mean[:], neg_inv_z[:], ALU.subtract, ALU.mult)
-        nc.vector.tensor_tensor(scattered[:].indirect(offsets[:]), dp[:], sig[:], ALU.mult)
-        final_scale = -OUT_SCALE
+        nc.vector.scalar_tensor_tensor(
+            weighted_dw[:], dw[:], neg_inv_z[:], neg_p[:, listed], ALU.mult, ALU.mult, accum_out=mean[:]
+        )
+        neg_dp = sb.tile([P, SLOTS], F32, name="neg_dp")
+        nc.vector.tensor_scalar(neg_dp[:], dw[:], mean[:], neg_inv_z[:], ALU.subtract, ALU.mult)
 
-        for h, (lo, hi) in enumerate([(0, 512), (512, 1024)]):
-            y = sb.tile([P, hi - lo], F32, name="y%d" % h)
-            nc.vector.scalar_tensor_tensor(y[:], scattered[:, lo:hi], final_scale, old_sb[:, lo:hi], ALU.mult, ALU.add)
-            [nc.sync, nc.scalar][h % 2].dma_start(out=out[:, lo:hi], in_=y[:])
+        nc.vector.tensor_tensor(neg_s1[:].indirect(offsets[:]), neg_dp[:], sigmoid_x[:], ALU.mult)
+
+        for piece, queue in enumerate((nc.sync, nc.scalar)):
+            cols = slice(piece * STORE_PIECE, (piece + 1) * STORE_PIECE)
+            y = sb.tile([P, STORE_PIECE], F32, name="y%d" % piece)
+            nc.vector.scalar_tensor_tensor(y[:], neg_s1[:, cols], -OUT_SCALE, old_sb[:, cols], ALU.mult, ALU.add)
+            queue.dma_start(out=out[:, cols], in_=y[:])

from contextlib import ExitStack

import concourse.mybir as mybir

F32 = mybir.dt.float32
BF16 = mybir.dt.bfloat16
I32 = mybir.dt.int32
U32 = mybir.dt.uint32
U16 = mybir.dt.uint16
U8 = mybir.dt.uint8
FP8X4 = mybir.dt.float8_e4m3fn_x4
ALU = mybir.AluOpType
ACT = mybir.ActivationFunctionType

P = 128
PACK = 4
T = 1024
SLOTS = 512
PADDED_SLOTS = SLOTS + 8
BANK = 512
OUT_SCALE = 1024.0
LN_FLOOR = 2.0**-63
NEVER_THE_MINIMUM = 2.0**100

SCORE_PIECE = 256
VALS_CHUNKS = (128, 256, 256, 256, 128)
SCALAR_CHUNK = 1
STORE_PIECE = 512

FLOPS = 2 * 2 * P * (P * PACK) * T


def interleave(copy, grouped, raw):
    copy(
        out=grouped[:].rearrange("p (c i) j -> p c j i", i=4),
        in_=raw[:].rearrange("p j (c i) -> p c j i", i=4),
    )


def quantize(nc, codes, scales, grouped):
    nc.vector.quantize_mx(out=codes[:].bitcast(FP8X4), scales=scales[:], in_=grouped[:].rearrange("p c j -> p (c j)"))


def tile_attend_bspotlight_heads_kernel(tc, query, keys_words, keys_scales, gout, vals, th, reserve, old, offs, out):
    nc = tc.nc
    last_chunk = len(VALS_CHUNKS) - 1
    chunk_starts = [sum(VALS_CHUNKS[:c]) for c in range(len(VALS_CHUNKS))]
    listed = slice(0, SLOTS)
    reserve_column = slice(SLOTS, SLOTS + 1)
    listed_and_reserve = slice(0, SLOTS + 1)

    with ExitStack() as ctx:
        sb = ctx.enter_context(tc.tile_pool(name="sb", bufs=1))
        ps = ctx.enter_context(tc.psum_pool(name="ps", bufs=1))

        offsets = sb.tile([P, SLOTS // 16], U16, name="offsets")
        k_scales = sb.tile([P, T], U8, name="k_scales", align_bytes=64)
        k_codes = sb.tile([P, T], U32, name="k_codes", align_bytes=64)
        for quadrant in range(4):
            nc.scalar.dma_start(
                out=k_scales[32 * quadrant : 32 * quadrant + 4, :].bitcast(I32),
                in_=keys_scales[0, 4 * quadrant : 4 * quadrant + 4, :].bitcast(I32),
            )
        th_col = sb.tile([P, 1], F32, name="th_col")
        nc.scalar.dma_start(out=th_col[:], in_=th)

        warm_in = sb.tile([P, 1], F32, name="warm_in")
        warm_out = sb.tile([P, 1], F32, name="warm_out")
        nc.vector.memset(warm_in[:], 0.0)
        nc.scalar.activation(warm_out[:], warm_in[:], ACT.Sigmoid)

        reserve_col = sb.tile([P, 1], F32, name="reserve_col")
        q_raw = sb.tile([P, PACK, P], F32, name="q_raw")
        g_raw = sb.tile([P, PACK, P], F32, name="g_raw")
        v_raw = [sb.tile([P, PACK, w], F32, name="v_raw%d" % c, align_bytes=64) for c, w in enumerate(VALS_CHUNKS)]
        old_sb = sb.tile([P, T], F32, name="old_sb")
        nc.sync.dma_start(out=q_raw[:], in_=query.rearrange("(p j) c -> p j c", j=PACK))
        nc.sync.dma_start(out=k_codes[:].bitcast(I32), in_=keys_words[0].rearrange("p c j -> p (c j)").bitcast(I32))
        nc.sync.dma_start(out=g_raw[:], in_=gout.rearrange("(p j) c -> p j c", j=PACK))
        nc.sync.dma_start(offsets[:], offs)
        vals_rows = vals.rearrange("(p j) c -> p j c", j=PACK)
        for c, w in enumerate(VALS_CHUNKS):
            nc.sync.dma_start(out=v_raw[c][:], in_=vals_rows[:, :, chunk_starts[c] : chunk_starts[c] + w])
        nc.sync.dma_start(out=reserve_col[:], in_=reserve)
        nc.sync.dma_start(out=old_sb[:], in_=old)

        neg_s1 = sb.tile([P, T], F32, name="neg_s1")
        nc.vector.memset(neg_s1[:], 0.0)
        neg_a = sb.tile([P, PADDED_SLOTS], F32, name="neg_a")
        ln_sigmoid = sb.tile([P, PADDED_SLOTS], F32, name="ln_sigmoid")
        nc.vector.memset(neg_a[:, reserve_column], NEVER_THE_MINIMUM)

        q_grouped = sb.tile([P, P, PACK], BF16, name="q_grouped", align_bytes=64)
        q_codes = sb.tile([P, P], U32, name="q_codes", align_bytes=64)
        q_scales = sb.tile([P, P], U8, name="q_scales", align_bytes=64)
        interleave(nc.vector.tensor_copy, q_grouped, q_raw)
        quantize(nc, q_codes, q_scales, q_grouped)
        g_grouped = sb.tile([P, P, PACK], BF16, name="g_grouped", align_bytes=64)
        g_codes = sb.tile([P, P], U32, name="g_codes", align_bytes=64)
        g_scales = sb.tile([P, P], U8, name="g_scales", align_bytes=64)
        interleave(nc.vector.tensor_copy, g_grouped, g_raw)
        quantize(nc, g_codes, g_scales, g_grouped)

        a = sb.tile([P, T], F32, name="a", align_bytes=64)
        for piece in range(T // SCORE_PIECE):
            cols = slice(piece * SCORE_PIECE, (piece + 1) * SCORE_PIECE)
            a_bank = ps.tile([P, BANK], F32, name="a_bank%d" % piece)
            nc.tensor.matmul_mx(
                out=a_bank[:, 0:SCORE_PIECE],
                lhsT=q_codes[:].bitcast(FP8X4),
                lhsT_scale=q_scales[:],
                rhs=k_codes[:, cols].bitcast(FP8X4),
                rhs_scale=k_scales[:, cols],
                start=True,
                stop=True,
            )
            copy = nc.vector.tensor_copy if piece == 0 else nc.scalar.copy
            copy(out=a[:, cols], in_=a_bank[:, 0:SCORE_PIECE])

        nc.vector.tensor_scalar(neg_a[:, listed], a[:].indirect(offsets[:]), -1.0, 0.0, ALU.mult, ALU.add)

        c_banks = []
        bank_starts = []
        for c, w in enumerate(VALS_CHUNKS):
            v_grouped = sb.tile([P, w, PACK], BF16, name="v_grouped%d" % c, align_bytes=64)
            interleave(nc.scalar.copy if c == SCALAR_CHUNK else nc.vector.tensor_copy, v_grouped, v_raw[c])
            v_codes = sb.tile([P, w], U32, name="v_codes%d" % c, align_bytes=64)
            v_scales = sb.tile([P, w], U8, name="v_scales%d" % c, align_bytes=64)
            quantize(nc, v_codes, v_scales, v_grouped)
            if c != SCALAR_CHUNK:
                c_banks.append(ps.tile([P, BANK], F32, name="c_bank%d" % c))
                bank_starts.append(chunk_starts[c])
            at = chunk_starts[c] - bank_starts[-1]
            nc.tensor.matmul_mx(
                out=c_banks[-1][:, at : at + w],
                lhsT=g_codes[:].bitcast(FP8X4),
                lhsT_scale=g_scales[:],
                rhs=v_codes[:].bitcast(FP8X4),
                rhs_scale=v_scales[:],
                start=True,
                stop=True,
            )

        sigmoid_neg_x = sb.tile([P, SLOTS], F32, name="sigmoid_neg_x", tag="v_raw%d" % SCALAR_CHUNK, align_bytes=64)
        nc.scalar.activation(sigmoid_neg_x[:], neg_a[:, listed], ACT.Sigmoid, bias=th_col[:])
        nc.scalar.activation(ln_sigmoid[:, listed], sigmoid_neg_x[:], ACT.Ln, bias=LN_FLOOR)

        c0 = sb.tile([P, T], F32, name="c0", align_bytes=64)
        for bank, lo, hi in zip(c_banks, bank_starts, bank_starts[1:] + [T]):
            nc.scalar.copy(out=c0[:, lo:hi], in_=bank[:, 0 : hi - lo])

        neg_th = sb.tile([P, 1], F32, name="neg_th")
        nc.vector.tensor_scalar(neg_th[:], th_col[:], -1.0, 0.0, ALU.mult, ALU.add)
        nc.vector.tensor_scalar(ln_sigmoid[:, reserve_column], reserve_col[:], -1.0, 0.0, ALU.mult, ALU.add)

        neg_p = sb.tile([P, PADDED_SLOTS], F32, name="neg_p", tag="v_grouped%d" % last_chunk, align_bytes=64)
        neg_z = sb.tile([P, 1], F32, name="neg_z")
        neg_inv_z = sb.tile([P, 1], F32, name="neg_inv_z")
        nc.vector.scalar_tensor_tensor(
            neg_p[:, listed_and_reserve],
            neg_a[:, listed_and_reserve],
            th_col[:],
            ln_sigmoid[:, listed_and_reserve],
            ALU.add,
            ALU.min,
            accum_out=neg_z[:],
        )

        sigmoid_x = sb.tile([P, SLOTS], F32, name="sigmoid_x", tag="ln_sigmoid")
        nc.scalar.activation(sigmoid_x[:], neg_a[:, listed], ACT.Sigmoid, bias=neg_th[:], scale=-1.0)

        dw = sb.tile([P, SLOTS], F32, name="dw", align_bytes=64)
        nc.vector.tensor_copy(dw[:], c0[:].indirect(offsets[:]))
        nc.vector.reciprocal(neg_inv_z[:], neg_z[:])
        weighted_dw = sb.tile([P, SLOTS], F32, name="weighted_dw")
        mean = sb.tile([P, 1], F32, name="mean")
        nc.vector.scalar_tensor_tensor(
            weighted_dw[:], dw[:], neg_inv_z[:], neg_p[:, listed], ALU.mult, ALU.mult, accum_out=mean[:]
        )
        neg_dp = sb.tile([P, SLOTS], F32, name="neg_dp")
        nc.vector.tensor_scalar(neg_dp[:], dw[:], mean[:], neg_inv_z[:], ALU.subtract, ALU.mult)

        nc.vector.tensor_tensor(neg_s1[:].indirect(offsets[:]), neg_dp[:], sigmoid_x[:], ALU.mult)

        for piece, queue in enumerate((nc.sync, nc.scalar)):
            cols = slice(piece * STORE_PIECE, (piece + 1) * STORE_PIECE)
            y = sb.tile([P, STORE_PIECE], F32, name="y%d" % piece)
            nc.vector.scalar_tensor_tensor(y[:], neg_s1[:, cols], -OUT_SCALE, old_sb[:, cols], ALU.mult, ALU.add)
            queue.dma_start(out=out[:, cols], in_=y[:])
